import numpy as np
import ml_dtypes


def mxq(x, axis, fmt="e4m3"):
    dtype, down = {"e4m3": (ml_dtypes.float8_e4m3fn, 7), "e5m2": (ml_dtypes.float8_e5m2, 14)}[fmt]
    v = np.moveaxis(np.asarray(x, np.float32).astype(ml_dtypes.bfloat16).astype(np.float64), axis, -1)
    blocks = v.reshape(v.shape[:-1] + (-1, 32))
    amax = np.abs(blocks).max(-1, keepdims=True)
    byte = np.maximum(np.where(amax > 0, np.frexp(amax)[1] - 1 + 127, 0) - down, 1)
    scale = np.exp2(byte - 127.0)
    codes = (blocks / scale).astype(np.float32).astype(dtype).astype(np.float64)
    return np.moveaxis((codes * scale).reshape(v.shape), -1, axis)


WIDE = False


def mx_kscale(k):
    if not WIDE:
        return np.ones(k)
    levels = np.array([10, -10, 5, -5, 0])
    if k % 512:
        return np.exp2(np.random.permutation(np.resize(levels, k // 32))).repeat(32)
    a = np.empty((k // 512, 16))
    for p in range(k // 512):
        a[p, :8] = np.random.permutation(np.resize(levels, 8))
        for g in range(8):
            far = levels[np.abs(levels - a[p, g]) >= 10]
            a[p, g + 8] = far[np.random.randint(len(far))]
    return np.exp2(a.ravel()).repeat(32)


def f64(x):
    return np.asarray(x).astype(np.float64)


def striped(idx):
    return np.tile(idx.reshape(-1, 16).T, (8, 1)).astype(np.uint16)


def unstriped(offs):
    return offs[:16].T.reshape(-1).astype(np.int64)


def striped8(idx):
    return np.concatenate([x.reshape(-1, 16).T for x in idx]).astype(np.uint16)


def runs(offs, k):
    lists = np.stack([offs[16 * r : 16 * r + 16].T.reshape(-1) for r in range(8)]).astype(np.int64)
    return lists[np.arange(k) % 512 // 64]


def pack_weight(w):
    k, n = w.shape
    w = f64(np.asarray(w, np.float32).astype(ml_dtypes.bfloat16)).reshape(k // 32, 32, n)
    amax = np.abs(w).max(1)
    byte = np.clip(np.where(amax > 0, np.frexp(amax)[1] - 1 + 127 - 7, 1), 1, 254)
    scaled = (w * np.exp2(127.0 - byte)[:, None, :]).reshape(k, n).astype(np.float32)
    words = np.ascontiguousarray(scaled.reshape(k // 512, 128, 4, n).transpose(0, 1, 3, 2)).astype(ml_dtypes.float8_e4m3fn).view(np.uint8)
    return words, np.ascontiguousarray(byte.astype(np.uint8).reshape(k // 512, 16, n))


def unpack_weight(words, scales):
    g, p, n, _ = words.shape
    vals = np.ascontiguousarray(words).view(ml_dtypes.float8_e4m3fn).astype(np.float64) * np.repeat(np.exp2(scales.astype(np.float64) - 127.0), 8, axis=1)[..., None]
    return vals.transpose(0, 1, 3, 2).reshape(g * 512, n)


def sigmoid(v):
    return 1.0 / (1.0 + np.exp(-np.maximum(v, -700.0)))


K, T, S, V, H, W = 512, 2048, 512, 512, 512, 256


def setup_inputs():
    n = np.random.standard_normal
    s = mx_kscale(K)[:, None]
    u = mx_kscale(S)
    packed_xT = pack_weight(n((K, T)) * s)
    perm = np.stack([np.random.permutation(V) for _ in range(8)])
    return {
        "x_words": packed_xT[0],
        "x_scales": packed_xT[1],
        "w1": (n((K, H)) / np.sqrt(K) / s).astype(np.float32),
        "w2": (n((K, H)) / np.sqrt(K) / s).astype(np.float32),
        "w3": (n((K, H)) / np.sqrt(K) / s).astype(np.float32),
        "ga": (np.random.uniform(0.5, 1.5, (H, 1)) * u[:, None]).astype(np.float32),
        "gb": (np.random.uniform(0.5, 1.5, (H, 1)) / u[:, None]).astype(np.float32),
        "offs": striped(np.random.permutation(T)[:S]),
        "two": striped(np.random.permutation(T)[:S]),
        "n1": striped8(np.stack([np.random.permutation(S) for _ in range(8)])),
        "n2": striped8(np.stack([np.random.permutation(S) for _ in range(8)])),
        "n3": striped8(np.stack([np.random.permutation(S) for _ in range(8)])),
        "n4": striped8(np.stack([np.random.permutation(S) for _ in range(8)])),
        "three": striped(np.random.permutation(T)[:V]),
        "n5": striped8(perm[:, :W]),
        "n6": striped8(perm[:, W:]),
        "n7": striped8(np.stack([np.random.permutation(V) for _ in range(8)])),
        "n8": striped8(np.stack([np.random.permutation(V) for _ in range(8)])),
    }


def reference(x_words, x_scales, w1, w2, w3, ga, gb, offs, two, n1, n2, n3, n4, three, n5, n6, n7, n8):
    xq = unpack_weight(x_words, x_scales)[:, unstriped(offs)]
    y = mxq(f64(w1), 0, "e4m3").T @ xq
    x_two = unpack_weight(x_words, x_scales)[:, unstriped(two)]
    d = mxq(f64(w2), 0, "e4m3").T @ x_two
    z = f64(ga) * (np.maximum(y[np.arange(H)[:, None], runs(n1, H)] + d[np.arange(H)[:, None], runs(n3, H)], y[np.arange(H)[:, None], runs(n2, H)] + d[np.arange(H)[:, None], runs(n4, H)]))
    x_three = unpack_weight(x_words, x_scales)[:, unstriped(three)]
    b = mxq(f64(w3), 0, "e4m3").T @ x_three
    pa = b[np.arange(H)[:, None], runs(n5, H)]
    pb = b[np.arange(H)[:, None], runs(n6, H)]
    rb = pa - pb
    ra = 0.75 * (pa + pb)
    ds = np.zeros((H, V))
    ds[np.arange(H)[:, None], runs(n5, H)] = ra
    dt = ds.copy()
    dt[np.arange(H)[:, None], runs(n6, H)] = rb
    z2 = f64(gb) * dt
    s = 0.0625 * ((mxq(z, 0, "e4m3").T @ mxq(z2, 0, "e4m3")))
    return np.maximum(s * (sigmoid(s[np.arange(S)[:, None], runs(n7, S)])), s[np.arange(S)[:, None], runs(n8, S)])

@@ -1,0 +1,228 @@
+from contextlib import ExitStack
+
+import concourse.mybir as mybir
+
+F32 = mybir.dt.float32
+BF16 = mybir.dt.bfloat16
+I32 = mybir.dt.int32
+U32 = mybir.dt.uint32
+U16 = mybir.dt.uint16
+U8 = mybir.dt.uint8
+FP8X4 = mybir.dt.float8_e4m3fn_x4
+ALU = mybir.AluOpType
+ACT = mybir.ActivationFunctionType
+
+P = 128
+PACK = 4
+T = 2048
+N = 512
+PAIRS = 256
+WIDE = 2 * N
+
+FLOPS = 4 * 2 * 512 * 512 * 512
+
+
+def tile_picked_twkpathbhaargmax_none_p_kernel(
+    tc, x_words, x_scales, w1, w2, w3, ga, gb, offs, two, n1, n2, n3, n4, three, n5, n6, n7, n8, out
+):
+    nc = tc.nc
+    with ExitStack() as ctx:
+        lists = ctx.enter_context(tc.tile_pool(name="lists", bufs=1))
+        keep = ctx.enter_context(tc.tile_pool(name="keep", bufs=1))
+        psum = ctx.enter_context(tc.psum_pool(name="psum", bufs=8))
+
+        def load_list(src, name):
+            tile = lists.tile(list(src.shape), U16, name=name)
+            nc.sync.dma_start(tile[:], src)
+            return tile
+
+        def load_weight(src, name):
+            tile = keep.tile([P, PACK, N], F32, name=name)
+            nc.sync.dma_start(out=tile[:], in_=src.rearrange("(p j) c -> p j c", j=PACK))
+            return tile
+
+        warm = keep.tile([P, 2], F32, name="warm")
+        nc.gpsimd.memset(warm[:, 0:1], 0.0)
+        nc.scalar.activation(warm[:, 1:2], warm[:, 0:1], ACT.Sigmoid)
+
+        x_bytes = keep.tile([P, T], U8, name="x_bytes", align_bytes=64)
+        nc.vector.memset(x_bytes[:].bitcast(I32), 0)
+        l_three = load_list(three, "l_three")
+        for q in range(4):
+            nc.sync.dma_start(
+                out=x_bytes[32 * q : 32 * q + 4, :].bitcast(I32),
+                in_=x_scales[0, 4 * q : 4 * q + 4, :].bitcast(I32),
+            )
+        l_offs = load_list(offs, "l_offs")
+        l_two = load_list(two, "l_two")
+        raw3 = load_weight(w3, "raw3")
+        x_codes = keep.tile([P, T], U32, name="x_codes", align_bytes=64)
+        nc.sync.dma_start(
+            out=x_codes[:].bitcast(I32), in_=x_words[0].rearrange("p n t -> p (n t)").bitcast(I32)
+        )
+        l5 = load_list(n5, "l5")
+        l6 = load_list(n6, "l6")
+        raw1 = load_weight(w1, "raw1")
+        raw2 = load_weight(w2, "raw2")
+        l1 = load_list(n1, "l1")
+        l2 = load_list(n2, "l2")
+        l3 = load_list(n3, "l3")
+        l4 = load_list(n4, "l4")
+        l7 = load_list(n7, "l7")
+        l8 = load_list(n8, "l8")
+
+        ga_sb = keep.tile([P, PACK], F32, name="ga_sb")
+        gb_sb = keep.tile([P, PACK], F32, name="gb_sb")
+        nc.gpsimd.dma_start(out=ga_sb[:], in_=ga.rearrange("(p t) o -> p (t o)", t=PACK))
+        nc.gpsimd.dma_start(out=gb_sb[:], in_=gb.rearrange("(p t) o -> p (t o)", t=PACK))
+        step = keep.tile([P, PACK], F32, name="step")
+        sign = keep.tile([P, PACK], F32, name="sign")
+        ga_abs = keep.tile([P, PACK], F32, name="ga_abs")
+        gb_signed = keep.tile([P, PACK], F32, name="gb_signed")
+        nc.gpsimd.tensor_scalar(step[:], ga_sb[:], 0.0, 2.0, ALU.is_ge, ALU.mult)
+        nc.gpsimd.tensor_scalar(sign[:], step[:], 1.0, -1.0, ALU.mult, ALU.add)
+        nc.gpsimd.tensor_tensor(gb_signed[:], gb_sb[:], sign[:], ALU.mult)
+        nc.gpsimd.tensor_tensor(ga_abs[:], ga_sb[:], sign[:], ALU.mult)
+
+        def pick_bytes(lst, name):
+            tile = keep.tile([P, N], U8, name=name, align_bytes=64)
+            nc.vector.tensor_copy(tile[:], x_bytes[:].indirect(lst[:]))
+            return tile
+
+        def pick_codes(lst, name):
+            tile = keep.tile([P, N], U32, name=name, align_bytes=64)
+            nc.vector.tensor_copy(tile[:], x_codes[:].indirect(lst[:]))
+            return tile
+
+        def round_weight(raw, name):
+            grouped = keep.tile([P, PACK * N], BF16, name=name, tag=name, align_bytes=64)
+            src = raw[:].rearrange("p j (m h e) -> p h m j e", h=2, e=2)
+            dst = grouped[:].rearrange("p (h e m j) -> p h m j e", h=2, e=2, j=PACK)
+            for h in range(2):
+                nc.scalar.copy(dst[:, h], src[:, h])
+            return grouped
+
+        def quantise(grouped, name, parts, tag=None):
+            width = grouped.shape[1] // PACK
+            codes = keep.tile([P, width], U32, name=name + "_codes", tag=tag or name + "_codes", align_bytes=64)
+            scales = keep.tile([P, width], U8, name=name + "_scales", align_bytes=64)
+            w = width // parts
+            for i in range(parts):
+                nc.vector.quantize_mx(
+                    out=codes[:, i * w : (i + 1) * w].bitcast(FP8X4),
+                    scales=scales[:, i * w : (i + 1) * w],
+                    in_=grouped[:, PACK * i * w : PACK * (i + 1) * w],
+                )
+            return codes, scales
+
+        def product(lhs, cols, rhs):
+            acc = psum.tile([P, N], F32, name="acc")
+            nc.tensor.matmul_mx(
+                out=acc[:],
+                lhsT=lhs[0][:, cols].bitcast(FP8X4),
+                lhsT_scale=lhs[1][:, cols],
+                rhs=rhs[0][:].bitcast(FP8X4),
+                rhs_scale=rhs[1][:],
+                start=True,
+                stop=True,
+            )
+            return acc
+
+        bytes_three = pick_bytes(l_three, "bytes_three")
+        bytes_offs = pick_bytes(l_offs, "bytes_offs")
+        bytes_two = pick_bytes(l_two, "bytes_two")
+        q3 = quantise(round_weight(raw3, "grouped3"), "q3", 2)
+        x_three = (pick_codes(l_three, "codes_three"), bytes_three)
+        x_offs = (pick_codes(l_offs, "codes_offs"), bytes_offs)
+        x_two = (pick_codes(l_two, "codes_two"), bytes_two)
+
+        pairs = []
+        for t in range(PACK):
+            acc = product(q3, slice(P * t, P * (t + 1)), x_three)
+            b = keep.tile([P, N], F32, name="b%d" % t, tag="b%d" % t, align_bytes=64)
+            nc.scalar.activation(b[:], acc[:], ACT.Copy, scale=gb_signed[:, t : t + 1])
+            pa = keep.tile([P, PAIRS], F32, name="pa%d" % t)
+            pb_neg = keep.tile([P, PAIRS], F32, name="pb_neg%d" % t)
+            nc.vector.tensor_copy(pa[:], b[:].indirect(l5[:]))
+            nc.vector.tensor_scalar(pb_neg[:], b[:].indirect(l6[:]), -1.0, 0.0, ALU.mult, ALU.add)
+            pa75 = keep.tile([P, PAIRS], F32, name="pa75_%d" % t)
+            pb75 = keep.tile([P, PAIRS], F32, name="pb75_%d" % t)
+            nc.scalar.mul(pa75[:], pa[:], 0.75)
+            nc.scalar.mul(pb75[:], pb_neg[:], -0.75)
+            pairs.append((pa, pb_neg, pa75, pb75))
+
+        q1 = quantise(round_weight(raw1, "grouped1"), "q1", 1)
+        q2 = quantise(round_weight(raw2, "grouped2"), "q2", 1)
+
+        y, d = [], []
+        for t in range(PACK):
+            for res, q, x, nm in ((y, q1, x_offs, "y"), (d, q2, x_two, "d")):
+                acc = product(q, slice(P * t, P * (t + 1)), x)
+                win = keep.tile([P, WIDE], F32, name="%s%d" % (nm, t))
+                nc.scalar.activation(win[:, :N], acc[:], ACT.Copy, scale=ga_abs[:, t : t + 1])
+                res.append(win)
+
+        dt_tags = ("b3", "b2", "grouped1", "grouped2")
+        dt = [keep.tile([P, N], F32, name="dt%d" % t, tag=dt_tags[t], align_bytes=64) for t in range(PACK)]
+
+        def put_difference(t):
+            nc.vector.tensor_tensor(dt[t][:].indirect(l6[:]), pairs[t][0][:], pairs[t][1][:], ALU.add)
+
+        def put_sum(t):
+            nc.vector.tensor_tensor(dt[t][:].indirect(l5[:]), pairs[t][2][:], pairs[t][3][:], ALU.add)
+
+        put_difference(0)
+        for t in range(1, PACK):
+            put_difference(t)
+            put_sum(t - 1)
+        put_sum(PACK - 1)
+
+        z2_planes = keep.tile([P, PACK, N], BF16, name="z2_planes", tag="q2_codes", align_bytes=64)
+        for t in range(PACK):
+            nc.scalar.copy(z2_planes[:, t, :], dt[t][:])
+        z2_grouped = keep.tile([P, PACK * N], BF16, name="z2_grouped", align_bytes=64)
+        nc.scalar.copy(
+            z2_grouped[:].rearrange("p (c i t) -> p c t i", i=4, t=PACK),
+            z2_planes[:].rearrange("p t (c i) -> p c t i", i=4),
+        )
+
+        first = keep.tile([P, PACK, N], F32, name="first")
+        second = keep.tile([P, PACK, N], F32, name="second")
+        for t in range(PACK):
+            y1 = keep.tile([P, N], F32, name="y1_%d" % t, tag="y1_%d" % t, align_bytes=64)
+            y2 = keep.tile([P, N], F32, name="y2_%d" % t)
+            nc.vector.tensor_copy(y1[:], y[t][:].indirect(l1[:]))
+            nc.vector.tensor_copy(y2[:], y[t][:].indirect(l2[:]))
+            nc.vector.tensor_tensor(first[:, t, :], d[t][:].indirect(l3[:]), y1[:], ALU.add)
+            nc.vector.tensor_tensor(second[:, t, :], d[t][:].indirect(l4[:]), y2[:], ALU.add)
+
+        qz2 = quantise(z2_grouped, "moving", 1, tag="y1_2")
+
+        first_v = first[:].rearrange("p t (g u r) -> p u g t r", u=4, r=4)
+        second_v = second[:].rearrange("p t (g u r) -> p u g t r", u=4, r=4)
+        z_grouped = []
+        for u in range(4):
+            zg = keep.tile([P, N], BF16, name="z_grouped%d" % u, align_bytes=64)
+            nc.vector.tensor_tensor(
+                zg[:].rearrange("p (g r t) -> p g t r", r=4, t=PACK), first_v[:, u], second_v[:, u], ALU.max
+            )
+            z_grouped.append(zg)
+        out_v = out.rearrange("(g u r) v -> u g r v", u=4, r=4)
+        scores = []
+        for u in range(4):
+            qz = quantise(z_grouped[u], "qz%d" % u, 1)
+            acc = product(qz, slice(0, P), qz2)
+            s = keep.tile([P, WIDE], F32, name="s%d" % u)
+            nc.scalar.mul(s[:, :N], acc[:], 0.0625)
+            gate = keep.tile([P, N], F32, name="gate%d" % u)
+            nc.scalar.activation(gate[:], s[:].indirect(l7[:]), ACT.Sigmoid)
+            scores.append((s, gate))
+        for u in range(4):
+            s, gate = scores[u]
+            s8 = keep.tile([P, N], F32, name="s8_%d" % u)
+            gated = keep.tile([P, N], F32, name="gated%d" % u)
+            res = keep.tile([P, N], F32, name="res%d" % u)
+            nc.vector.tensor_copy(s8[:], s[:].indirect(l8[:]))
+            nc.vector.tensor_tensor(gated[:], s[:, :N], gate[:], ALU.mult)
+            nc.vector.tensor_tensor(res[:], gated[:], s8[:], ALU.max)
+            nc.sync.dma_start(out=out_v[u], in_=res[:])

@@ -29,6 +29,7 @@ def tile_picked_twkpathbhaargmax_none_p_kernel(
     with ExitStack() as ctx:
         lists = ctx.enter_context(tc.tile_pool(name="lists", bufs=1))
         keep = ctx.enter_context(tc.tile_pool(name="keep", bufs=1))
+        share = ctx.enter_context(tc.tile_pool(name="share", bufs=1))
         psum = ctx.enter_context(tc.psum_pool(name="psum", bufs=8))
 
         def load_list(src, name):
@@ -41,25 +42,31 @@ def tile_picked_twkpathbhaargmax_none_p_kernel(
             nc.sync.dma_start(out=tile[:], in_=src.rearrange("(p j) c -> p j c", j=PACK))
             return tile
 
+        x_bytes = keep.tile([P, T], U8, name="x_bytes", align_bytes=64)
+        nc.vector.memset(x_bytes[:].bitcast(I32), 0)
         warm = keep.tile([P, 2], F32, name="warm")
         nc.gpsimd.memset(warm[:, 0:1], 0.0)
         nc.scalar.activation(warm[:, 1:2], warm[:, 0:1], ACT.Sigmoid)
 
-        x_bytes = keep.tile([P, T], U8, name="x_bytes", align_bytes=64)
-        nc.vector.memset(x_bytes[:].bitcast(I32), 0)
         l_three = load_list(three, "l_three")
+        l_offs = load_list(offs, "l_offs")
+        l_two = load_list(two, "l_two")
         for q in range(4):
             nc.sync.dma_start(
                 out=x_bytes[32 * q : 32 * q + 4, :].bitcast(I32),
                 in_=x_scales[0, 4 * q : 4 * q + 4, :].bitcast(I32),
             )
-        l_offs = load_list(offs, "l_offs")
-        l_two = load_list(two, "l_two")
-        raw3 = load_weight(w3, "raw3")
         x_codes = keep.tile([P, T], U32, name="x_codes", align_bytes=64)
         nc.sync.dma_start(
             out=x_codes[:].bitcast(I32), in_=x_words[0].rearrange("p n t -> p (n t)").bitcast(I32)
         )
+        raw3 = []
+        for c in range(2):
+            part = keep.tile([P, PACK, N // 2], F32, name="raw3_%d" % c)
+            nc.sync.dma_start(
+                out=part[:], in_=w3.rearrange("(p j) c -> p j c", j=PACK)[:, :, c * N // 2 : (c + 1) * N // 2]
+            )
+            raw3.append(part)
         l5 = load_list(n5, "l5")
         l6 = load_list(n6, "l6")
         raw1 = load_weight(w1, "raw1")
@@ -89,30 +96,20 @@ def tile_picked_twkpathbhaargmax_none_p_kernel(
             nc.vector.tensor_copy(tile[:], x_bytes[:].indirect(lst[:]))
             return tile
 
-        def pick_codes(lst, name):
-            tile = keep.tile([P, N], U32, name=name, align_bytes=64)
+        def pick_codes(lst, name, tag=None):
+            tile = keep.tile([P, N], U32, name=name, tag=tag or name, align_bytes=64)
             nc.vector.tensor_copy(tile[:], x_codes[:].indirect(lst[:]))
             return tile
 
-        def round_weight(raw, name):
-            grouped = keep.tile([P, PACK * N], BF16, name=name, tag=name, align_bytes=64)
+        def round_half(raw, h, grouped):
             src = raw[:].rearrange("p j (m h e) -> p h m j e", h=2, e=2)
-            dst = grouped[:].rearrange("p (h e m j) -> p h m j e", h=2, e=2, j=PACK)
-            for h in range(2):
-                nc.scalar.copy(dst[:, h], src[:, h])
-            return grouped
+            nc.scalar.copy(grouped.rearrange("p (e m j) -> p m j e", e=2, j=PACK), src[:, h])
 
-        def quantise(grouped, name, parts, tag=None):
+        def quantise(grouped, name, tag=None):
             width = grouped.shape[1] // PACK
             codes = keep.tile([P, width], U32, name=name + "_codes", tag=tag or name + "_codes", align_bytes=64)
             scales = keep.tile([P, width], U8, name=name + "_scales", align_bytes=64)
-            w = width // parts
-            for i in range(parts):
-                nc.vector.quantize_mx(
-                    out=codes[:, i * w : (i + 1) * w].bitcast(FP8X4),
-                    scales=scales[:, i * w : (i + 1) * w],
-                    in_=grouped[:, PACK * i * w : PACK * (i + 1) * w],
-                )
+            nc.vector.quantize_mx(out=codes[:].bitcast(FP8X4), scales=scales[:], in_=grouped[:])
             return codes, scales
 
         def product(lhs, cols, rhs):
@@ -131,39 +128,58 @@ def tile_picked_twkpathbhaargmax_none_p_kernel(
         bytes_three = pick_bytes(l_three, "bytes_three")
         bytes_offs = pick_bytes(l_offs, "bytes_offs")
         bytes_two = pick_bytes(l_two, "bytes_two")
-        q3 = quantise(round_weight(raw3, "grouped3"), "q3", 2)
         x_three = (pick_codes(l_three, "codes_three"), bytes_three)
         x_offs = (pick_codes(l_offs, "codes_offs"), bytes_offs)
-        x_two = (pick_codes(l_two, "codes_two"), bytes_two)
+        grouped3 = [
+            keep.tile([P, 2 * N], BF16, name="grouped3_%d" % h, tag="grouped3_%d" % h, align_bytes=64)
+            for h in range(2)
+        ]
+        for c in range(2):
+            src = raw3[c][:].rearrange("p j (m h e) -> p h m j e", h=2, e=2)
+            for h in range(2):
+                dst = grouped3[h][:].rearrange("p (e c m j) -> p c m j e", e=2, c=2, j=PACK)
+                nc.scalar.copy(dst[:, c], src[:, h])
+        q3 = [quantise(grouped3[h], "q3_%d" % h) for h in range(2)]
+        x_two = (pick_codes(l_two, "codes_two", tag="grouped3_0"), bytes_two)
 
-        pairs = []
+        fetched_pairs = []
         for t in range(PACK):
-            acc = product(q3, slice(P * t, P * (t + 1)), x_three)
-            b = keep.tile([P, N], F32, name="b%d" % t, tag="b%d" % t, align_bytes=64)
-            nc.scalar.activation(b[:], acc[:], ACT.Copy, scale=gb_signed[:, t : t + 1])
+            acc = product(q3[t // 2], slice(P * (t % 2), P * (t % 2 + 1)), x_three)
+            if t < PACK - 1:
+                b = keep.tile([P, N], F32, name="b%d" % t)
+            else:
+                b = share.tile([P, N], F32, name="b%d" % t, offset=16 * N + 2 * N, align_bytes=64)
+            nc.scalar.copy(b[:], acc[:])
             pa = keep.tile([P, PAIRS], F32, name="pa%d" % t)
             pb_neg = keep.tile([P, PAIRS], F32, name="pb_neg%d" % t)
             nc.vector.tensor_copy(pa[:], b[:].indirect(l5[:]))
             nc.vector.tensor_scalar(pb_neg[:], b[:].indirect(l6[:]), -1.0, 0.0, ALU.mult, ALU.add)
+            fetched_pairs.append((pa, pb_neg))
+
+        grouped12 = share.tile([P, 2 * PACK * N], BF16, name="grouped12", offset=0, align_bytes=64)
+        for i, raw in enumerate((raw1, raw2)):
+            for h in range(2):
+                round_half(raw, h, grouped12[:, (2 * i + h) * 2 * N : (2 * i + h + 1) * 2 * N])
+        pairs = []
+        for t in range(PACK):
+            pa, pb_neg = fetched_pairs[t]
             pa75 = keep.tile([P, PAIRS], F32, name="pa75_%d" % t)
             pb75 = keep.tile([P, PAIRS], F32, name="pb75_%d" % t)
             nc.scalar.mul(pa75[:], pa[:], 0.75)
             nc.scalar.mul(pb75[:], pb_neg[:], -0.75)
             pairs.append((pa, pb_neg, pa75, pb75))
-
-        q1 = quantise(round_weight(raw1, "grouped1"), "q1", 1)
-        q2 = quantise(round_weight(raw2, "grouped2"), "q2", 1)
+        q12 = quantise(grouped12, "q12")
 
         y, d = [], []
         for t in range(PACK):
-            for res, q, x, nm in ((y, q1, x_offs, "y"), (d, q2, x_two, "d")):
-                acc = product(q, slice(P * t, P * (t + 1)), x)
+            for res, c0, x, nm in ((y, 0, x_offs, "y"), (d, N, x_two, "d")):
+                acc = product(q12, slice(c0 + P * t, c0 + P * (t + 1)), x)
                 win = keep.tile([P, WIDE], F32, name="%s%d" % (nm, t))
                 nc.scalar.activation(win[:, :N], acc[:], ACT.Copy, scale=ga_abs[:, t : t + 1])
                 res.append(win)
 
-        dt_tags = ("b3", "b2", "grouped1", "grouped2")
-        dt = [keep.tile([P, N], F32, name="dt%d" % t, tag=dt_tags[t], align_bytes=64) for t in range(PACK)]
+        dt_offsets = (16 * N, 20 * N, 0, 4 * N)
+        dt = [share.tile([P, N], F32, name="dt%d" % t, offset=dt_offsets[t], align_bytes=64) for t in range(PACK)]
 
         def put_difference(t):
             nc.vector.tensor_tensor(dt[t][:].indirect(l6[:]), pairs[t][0][:], pairs[t][1][:], ALU.add)
@@ -177,9 +193,9 @@ def tile_picked_twkpathbhaargmax_none_p_kernel(
             put_sum(t - 1)
         put_sum(PACK - 1)
 
-        z2_planes = keep.tile([P, PACK, N], BF16, name="z2_planes", tag="q2_codes", align_bytes=64)
+        z2_planes = keep.tile([P, PACK, N], BF16, name="z2_planes", tag="q12_codes", align_bytes=64)
         for t in range(PACK):
-            nc.scalar.copy(z2_planes[:, t, :], dt[t][:])
+            nc.scalar.activation(z2_planes[:, t, :], dt[t][:], ACT.Copy, scale=gb_signed[:, t : t + 1])
         z2_grouped = keep.tile([P, PACK * N], BF16, name="z2_grouped", align_bytes=64)
         nc.scalar.copy(
             z2_grouped[:].rearrange("p (c i t) -> p c t i", i=4, t=PACK),
@@ -196,7 +212,7 @@ def tile_picked_twkpathbhaargmax_none_p_kernel(
             nc.vector.tensor_tensor(first[:, t, :], d[t][:].indirect(l3[:]), y1[:], ALU.add)
             nc.vector.tensor_tensor(second[:, t, :], d[t][:].indirect(l4[:]), y2[:], ALU.add)
 
-        qz2 = quantise(z2_grouped, "moving", 1, tag="y1_2")
+        qz2 = quantise(z2_grouped, "moving", tag="y1_1")
 
         first_v = first[:].rearrange("p t (g u r) -> p u g t r", u=4, r=4)
         second_v = second[:].rearrange("p t (g u r) -> p u g t r", u=4, r=4)
@@ -210,19 +226,42 @@ def tile_picked_twkpathbhaargmax_none_p_kernel(
         out_v = out.rearrange("(g u r) v -> u g r v", u=4, r=4)
         scores = []
         for u in range(4):
-            qz = quantise(z_grouped[u], "qz%d" % u, 1)
+            qz = quantise(z_grouped[u], "qz%d" % u)
             acc = product(qz, slice(0, P), qz2)
             s = keep.tile([P, WIDE], F32, name="s%d" % u)
             nc.scalar.mul(s[:, :N], acc[:], 0.0625)
             gate = keep.tile([P, N], F32, name="gate%d" % u)
-            nc.scalar.activation(gate[:], s[:].indirect(l7[:]), ACT.Sigmoid)
             scores.append((s, gate))
-        for u in range(4):
-            s, gate = scores[u]
-            s8 = keep.tile([P, N], F32, name="s8_%d" % u)
-            gated = keep.tile([P, N], F32, name="gated%d" % u)
+            if u > 0:
+                nc.scalar.activation(scores[u - 1][1][:], scores[u - 1][0][:].indirect(l7[:]), ACT.Sigmoid)
+        nc.scalar.activation(scores[3][1][:], scores[3][0][:].indirect(l7[:]), ACT.Sigmoid)
+        fetched, gated = [], []
+
+        def fetch(u):
+            tile = keep.tile([P, N], F32, name="fetched%d" % u)
+            nc.vector.tensor_copy(tile[:], scores[u][0][:].indirect(l8[:]))
+            fetched.append(tile)
+
+        def gate_scores(u, engine):
+            tile = keep.tile([P, N], F32, name="gated%d" % u)
+            engine.tensor_tensor(tile[:], scores[u][0][:, :N], scores[u][1][:], ALU.mult)
+            gated.append(tile)
+
+        def finish(u, parts):
             res = keep.tile([P, N], F32, name="res%d" % u)
-            nc.vector.tensor_copy(s8[:], s[:].indirect(l8[:]))
-            nc.vector.tensor_tensor(gated[:], s[:, :N], gate[:], ALU.mult)
-            nc.vector.tensor_tensor(res[:], gated[:], s8[:], ALU.max)
-            nc.sync.dma_start(out=out_v[u], in_=res[:])
+            for c in range(0, N, N // parts):
+                cols = slice(c, c + N // parts)
+                nc.vector.tensor_tensor(res[:, cols], gated[u][:, cols], fetched[u][:, cols], ALU.max)
+                nc.sync.dma_start(out=out_v[u][:, :, cols], in_=res[:, cols])
+
+        for u in range(3):
+            gate_scores(u, nc.gpsimd)
+        fetch(0)
+        fetch(1)
+        fetch(2)
+        finish(0, 1)
+        fetch(3)
+        finish(1, 1)
+        gate_scores(3, nc.vector)
+        finish(2, 1)
+        finish(3, 2)

@@ -37,8 +37,8 @@ def tile_picked_twkpathbhaargmax_none_p_kernel(
             nc.sync.dma_start(tile[:], src)
             return tile
 
-        def load_weight(src, name):
-            tile = keep.tile([P, PACK, N], F32, name=name)
+        def load_weight(src, name, pool, **place):
+            tile = pool.tile([P, PACK, N], F32, name=name, **place)
             nc.sync.dma_start(out=tile[:], in_=src.rearrange("(p j) c -> p j c", j=PACK))
             return tile
 
@@ -69,8 +69,8 @@ def tile_picked_twkpathbhaargmax_none_p_kernel(
             raw3.append(part)
         l5 = load_list(n5, "l5")
         l6 = load_list(n6, "l6")
-        raw1 = load_weight(w1, "raw1")
-        raw2 = load_weight(w2, "raw2")
+        raw1 = load_weight(w1, "raw1", keep)
+        raw2 = load_weight(w2, "raw2", share, offset=0, align_bytes=64)
         l1 = load_list(n1, "l1")
         l2 = load_list(n2, "l2")
         l3 = load_list(n3, "l3")
@@ -96,8 +96,8 @@ def tile_picked_twkpathbhaargmax_none_p_kernel(
             nc.vector.tensor_copy(tile[:], x_bytes[:].indirect(lst[:]))
             return tile
 
-        def pick_codes(lst, name, tag=None):
-            tile = keep.tile([P, N], U32, name=name, tag=tag or name, align_bytes=64)
+        def pick_codes(lst, name, pool, **place):
+            tile = pool.tile([P, N], U32, name=name, align_bytes=64, **place)
             nc.vector.tensor_copy(tile[:], x_codes[:].indirect(lst[:]))
             return tile
 
@@ -128,8 +128,8 @@ def tile_picked_twkpathbhaargmax_none_p_kernel(
         bytes_three = pick_bytes(l_three, "bytes_three")
         bytes_offs = pick_bytes(l_offs, "bytes_offs")
         bytes_two = pick_bytes(l_two, "bytes_two")
-        x_three = (pick_codes(l_three, "codes_three"), bytes_three)
-        x_offs = (pick_codes(l_offs, "codes_offs"), bytes_offs)
+        x_three = (pick_codes(l_three, "codes_three", share, offset=18 * N), bytes_three)
+        x_offs = (pick_codes(l_offs, "codes_offs", keep), bytes_offs)
         grouped3 = [
             keep.tile([P, 2 * N], BF16, name="grouped3_%d" % h, tag="grouped3_%d" % h, align_bytes=64)
             for h in range(2)
@@ -140,15 +140,12 @@ def tile_picked_twkpathbhaargmax_none_p_kernel(
                 dst = grouped3[h][:].rearrange("p (e c m j) -> p c m j e", e=2, c=2, j=PACK)
                 nc.scalar.copy(dst[:, c], src[:, h])
         q3 = [quantise(grouped3[h], "q3_%d" % h) for h in range(2)]
-        x_two = (pick_codes(l_two, "codes_two", tag="grouped3_0"), bytes_two)
+        x_two = (pick_codes(l_two, "codes_two", keep, tag="grouped3_0"), bytes_two)
 
         fetched_pairs = []
         for t in range(PACK):
             acc = product(q3[t // 2], slice(P * (t % 2), P * (t % 2 + 1)), x_three)
-            if t < PACK - 1:
-                b = keep.tile([P, N], F32, name="b%d" % t)
-            else:
-                b = share.tile([P, N], F32, name="b%d" % t, offset=16 * N + 2 * N, align_bytes=64)
+            b = keep.tile([P, N], F32, name="b%d" % t)
             nc.scalar.copy(b[:], acc[:])
             pa = keep.tile([P, PAIRS], F32, name="pa%d" % t)
             pb_neg = keep.tile([P, PAIRS], F32, name="pb_neg%d" % t)
@@ -156,7 +153,7 @@ def tile_picked_twkpathbhaargmax_none_p_kernel(
             nc.vector.tensor_scalar(pb_neg[:], b[:].indirect(l6[:]), -1.0, 0.0, ALU.mult, ALU.add)
             fetched_pairs.append((pa, pb_neg))
 
-        grouped12 = share.tile([P, 2 * PACK * N], BF16, name="grouped12", offset=0, align_bytes=64)
+        grouped12 = keep.tile([P, 2 * PACK * N], BF16, name="grouped12", align_bytes=64)
         for i, raw in enumerate((raw1, raw2)):
             for h in range(2):
                 round_half(raw, h, grouped12[:, (2 * i + h) * 2 * N : (2 * i + h + 1) * 2 * N])
@@ -212,20 +209,25 @@ def tile_picked_twkpathbhaargmax_none_p_kernel(
             nc.vector.tensor_tensor(first[:, t, :], d[t][:].indirect(l3[:]), y1[:], ALU.add)
             nc.vector.tensor_tensor(second[:, t, :], d[t][:].indirect(l4[:]), y2[:], ALU.add)
 
-        qz2 = quantise(z2_grouped, "moving", tag="y1_1")
+        qz2 = quantise(z2_grouped, "moving", tag="y1_3")
 
         first_v = first[:].rearrange("p t (g u r) -> p u g t r", u=4, r=4)
         second_v = second[:].rearrange("p t (g u r) -> p u g t r", u=4, r=4)
         z_grouped = []
-        for u in range(4):
+
+        def larger_sum(u):
             zg = keep.tile([P, N], BF16, name="z_grouped%d" % u, align_bytes=64)
             nc.vector.tensor_tensor(
                 zg[:].rearrange("p (g r t) -> p g t r", r=4, t=PACK), first_v[:, u], second_v[:, u], ALU.max
             )
             z_grouped.append(zg)
+
+        larger_sum(0)
         out_v = out.rearrange("(g u r) v -> u g r v", u=4, r=4)
         scores = []
         for u in range(4):
+            if u + 1 < 4:
+                larger_sum(u + 1)
             qz = quantise(z_grouped[u], "qz%d" % u)
             acc = product(qz, slice(0, P), qz2)
             s = keep.tile([P, WIDE], F32, name="s%d" % u)
@@ -242,9 +244,11 @@ def tile_picked_twkpathbhaargmax_none_p_kernel(
             nc.vector.tensor_copy(tile[:], scores[u][0][:].indirect(l8[:]))
             fetched.append(tile)
 
-        def gate_scores(u, engine):
+        def gate_scores(u, parts):
             tile = keep.tile([P, N], F32, name="gated%d" % u)
-            engine.tensor_tensor(tile[:], scores[u][0][:, :N], scores[u][1][:], ALU.mult)
+            for c in range(0, N, N // parts):
+                cols = slice(c, c + N // parts)
+                nc.vector.tensor_tensor(tile[:, cols], scores[u][0][:, cols], scores[u][1][:, cols], ALU.mult)
             gated.append(tile)
 
         def finish(u, parts):
@@ -254,14 +258,10 @@ def tile_picked_twkpathbhaargmax_none_p_kernel(
                 nc.vector.tensor_tensor(res[:, cols], gated[u][:, cols], fetched[u][:, cols], ALU.max)
                 nc.sync.dma_start(out=out_v[u][:, :, cols], in_=res[:, cols])
 
-        for u in range(3):
-            gate_scores(u, nc.gpsimd)
         fetch(0)
-        fetch(1)
-        fetch(2)
-        finish(0, 1)
-        fetch(3)
-        finish(1, 1)
-        gate_scores(3, nc.vector)
-        finish(2, 1)
+        for u in range(3):
+            gate_scores(u, 1)
+            fetch(u + 1)
+            finish(u, 1)
+        gate_scores(3, 2)
         finish(3, 2)

from contextlib import ExitStack

import concourse.mybir as mybir

F32 = mybir.dt.float32
BF16 = mybir.dt.bfloat16
I32 = mybir.dt.int32
U32 = mybir.dt.uint32
U16 = mybir.dt.uint16
U8 = mybir.dt.uint8
FP8X4 = mybir.dt.float8_e4m3fn_x4
ALU = mybir.AluOpType
ACT = mybir.ActivationFunctionType

P = 128
PACK = 4
T = 2048
N = 512
PAIRS = 256
WIDE = 2 * N

FLOPS = 4 * 2 * 512 * 512 * 512


def tile_picked_twkpathbhaargmax_none_p_kernel(
    tc, x_words, x_scales, w1, w2, w3, ga, gb, offs, two, n1, n2, n3, n4, three, n5, n6, n7, n8, out
):
    nc = tc.nc
    with ExitStack() as ctx:
        lists = ctx.enter_context(tc.tile_pool(name="lists", bufs=1))
        keep = ctx.enter_context(tc.tile_pool(name="keep", bufs=1))
        share = ctx.enter_context(tc.tile_pool(name="share", bufs=1))
        psum = ctx.enter_context(tc.psum_pool(name="psum", bufs=8))

        def load_list(src, name):
            tile = lists.tile(list(src.shape), U16, name=name)
            nc.sync.dma_start(tile[:], src)
            return tile

        def load_weight(src, name, pool, **place):
            tile = pool.tile([P, PACK, N], F32, name=name, **place)
            nc.sync.dma_start(out=tile[:], in_=src.rearrange("(p j) c -> p j c", j=PACK))
            return tile

        x_bytes = keep.tile([P, T], U8, name="x_bytes", align_bytes=64)
        nc.vector.memset(x_bytes[:].bitcast(I32), 0)
        warm = keep.tile([P, 2], F32, name="warm")
        nc.gpsimd.memset(warm[:, 0:1], 0.0)
        nc.scalar.activation(warm[:, 1:2], warm[:, 0:1], ACT.Sigmoid)

        l_three = load_list(three, "l_three")
        l_offs = load_list(offs, "l_offs")
        l_two = load_list(two, "l_two")
        for q in range(4):
            nc.sync.dma_start(
                out=x_bytes[32 * q : 32 * q + 4, :].bitcast(I32),
                in_=x_scales[0, 4 * q : 4 * q + 4, :].bitcast(I32),
            )
        x_codes = keep.tile([P, T], U32, name="x_codes", align_bytes=64)
        nc.sync.dma_start(
            out=x_codes[:].bitcast(I32), in_=x_words[0].rearrange("p n t -> p (n t)").bitcast(I32)
        )
        raw3 = []
        for c in range(2):
            part = keep.tile([P, PACK, N // 2], F32, name="raw3_%d" % c)
            nc.sync.dma_start(
                out=part[:], in_=w3.rearrange("(p j) c -> p j c", j=PACK)[:, :, c * N // 2 : (c + 1) * N // 2]
            )
            raw3.append(part)
        l5 = load_list(n5, "l5")
        l6 = load_list(n6, "l6")
        raw1 = load_weight(w1, "raw1", keep)
        raw2 = load_weight(w2, "raw2", share, offset=0, align_bytes=64)
        l1 = load_list(n1, "l1")
        l2 = load_list(n2, "l2")
        l3 = load_list(n3, "l3")
        l4 = load_list(n4, "l4")
        l7 = load_list(n7, "l7")
        l8 = load_list(n8, "l8")

        ga_sb = keep.tile([P, PACK], F32, name="ga_sb")
        gb_sb = keep.tile([P, PACK], F32, name="gb_sb")
        nc.gpsimd.dma_start(out=ga_sb[:], in_=ga.rearrange("(p t) o -> p (t o)", t=PACK))
        nc.gpsimd.dma_start(out=gb_sb[:], in_=gb.rearrange("(p t) o -> p (t o)", t=PACK))
        step = keep.tile([P, PACK], F32, name="step")
        sign = keep.tile([P, PACK], F32, name="sign")
        ga_abs = keep.tile([P, PACK], F32, name="ga_abs")
        gb_signed = keep.tile([P, PACK], F32, name="gb_signed")
        nc.gpsimd.tensor_scalar(step[:], ga_sb[:], 0.0, 2.0, ALU.is_ge, ALU.mult)
        nc.gpsimd.tensor_scalar(sign[:], step[:], 1.0, -1.0, ALU.mult, ALU.add)
        nc.gpsimd.tensor_tensor(gb_signed[:], gb_sb[:], sign[:], ALU.mult)
        nc.gpsimd.tensor_tensor(ga_abs[:], ga_sb[:], sign[:], ALU.mult)

        def pick_bytes(lst, name):
            tile = keep.tile([P, N], U8, name=name, align_bytes=64)
            nc.vector.tensor_copy(tile[:], x_bytes[:].indirect(lst[:]))
            return tile

        def pick_codes(lst, name, pool, **place):
            tile = pool.tile([P, N], U32, name=name, align_bytes=64, **place)
            nc.vector.tensor_copy(tile[:], x_codes[:].indirect(lst[:]))
            return tile

        def round_half(raw, h, grouped):
            src = raw[:].rearrange("p j (m h e) -> p h m j e", h=2, e=2)
            nc.scalar.copy(grouped.rearrange("p (e m j) -> p m j e", e=2, j=PACK), src[:, h])

        def quantise(grouped, name, tag=None):
            width = grouped.shape[1] // PACK
            codes = keep.tile([P, width], U32, name=name + "_codes", tag=tag or name + "_codes", align_bytes=64)
            scales = keep.tile([P, width], U8, name=name + "_scales", align_bytes=64)
            nc.vector.quantize_mx(out=codes[:].bitcast(FP8X4), scales=scales[:], in_=grouped[:])
            return codes, scales

        def product(lhs, cols, rhs):
            acc = psum.tile([P, N], F32, name="acc")
            nc.tensor.matmul_mx(
                out=acc[:],
                lhsT=lhs[0][:, cols].bitcast(FP8X4),
                lhsT_scale=lhs[1][:, cols],
                rhs=rhs[0][:].bitcast(FP8X4),
                rhs_scale=rhs[1][:],
                start=True,
                stop=True,
            )
            return acc

        bytes_three = pick_bytes(l_three, "bytes_three")
        bytes_offs = pick_bytes(l_offs, "bytes_offs")
        bytes_two = pick_bytes(l_two, "bytes_two")
        x_three = (pick_codes(l_three, "codes_three", share, offset=18 * N), bytes_three)
        x_offs = (pick_codes(l_offs, "codes_offs", keep), bytes_offs)
        grouped3 = [
            keep.tile([P, 2 * N], BF16, name="grouped3_%d" % h, tag="grouped3_%d" % h, align_bytes=64)
            for h in range(2)
        ]
        for c in range(2):
            src = raw3[c][:].rearrange("p j (m h e) -> p h m j e", h=2, e=2)
            for h in range(2):
                dst = grouped3[h][:].rearrange("p (e c m j) -> p c m j e", e=2, c=2, j=PACK)
                nc.scalar.copy(dst[:, c], src[:, h])
        q3 = [quantise(grouped3[h], "q3_%d" % h) for h in range(2)]
        x_two = (pick_codes(l_two, "codes_two", keep, tag="grouped3_0"), bytes_two)

        fetched_pairs = []
        for t in range(PACK):
            acc = product(q3[t // 2], slice(P * (t % 2), P * (t % 2 + 1)), x_three)
            b = keep.tile([P, N], F32, name="b%d" % t)
            nc.scalar.copy(b[:], acc[:])
            pa = keep.tile([P, PAIRS], F32, name="pa%d" % t)
            pb_neg = keep.tile([P, PAIRS], F32, name="pb_neg%d" % t)
            nc.vector.tensor_copy(pa[:], b[:].indirect(l5[:]))
            nc.vector.tensor_scalar(pb_neg[:], b[:].indirect(l6[:]), -1.0, 0.0, ALU.mult, ALU.add)
            fetched_pairs.append((pa, pb_neg))

        grouped12 = keep.tile([P, 2 * PACK * N], BF16, name="grouped12", align_bytes=64)
        for i, raw in enumerate((raw1, raw2)):
            for h in range(2):
                round_half(raw, h, grouped12[:, (2 * i + h) * 2 * N : (2 * i + h + 1) * 2 * N])
        pairs = []
        for t in range(PACK):
            pa, pb_neg = fetched_pairs[t]
            pa75 = keep.tile([P, PAIRS], F32, name="pa75_%d" % t)
            pb75 = keep.tile([P, PAIRS], F32, name="pb75_%d" % t)
            nc.scalar.mul(pa75[:], pa[:], 0.75)
            nc.scalar.mul(pb75[:], pb_neg[:], -0.75)
            pairs.append((pa, pb_neg, pa75, pb75))
        q12 = quantise(grouped12, "q12")

        y, d = [], []
        for t in range(PACK):
            for res, c0, x, nm in ((y, 0, x_offs, "y"), (d, N, x_two, "d")):
                acc = product(q12, slice(c0 + P * t, c0 + P * (t + 1)), x)
                win = keep.tile([P, WIDE], F32, name="%s%d" % (nm, t))
                nc.scalar.activation(win[:, :N], acc[:], ACT.Copy, scale=ga_abs[:, t : t + 1])
                res.append(win)

        dt_offsets = (16 * N, 20 * N, 0, 4 * N)
        dt = [share.tile([P, N], F32, name="dt%d" % t, offset=dt_offsets[t], align_bytes=64) for t in range(PACK)]

        def put_difference(t):
            nc.vector.tensor_tensor(dt[t][:].indirect(l6[:]), pairs[t][0][:], pairs[t][1][:], ALU.add)

        def put_sum(t):
            nc.vector.tensor_tensor(dt[t][:].indirect(l5[:]), pairs[t][2][:], pairs[t][3][:], ALU.add)

        put_difference(0)
        for t in range(1, PACK):
            put_difference(t)
            put_sum(t - 1)
        put_sum(PACK - 1)

        z2_planes = keep.tile([P, PACK, N], BF16, name="z2_planes", tag="q12_codes", align_bytes=64)
        for t in range(PACK):
            nc.scalar.activation(z2_planes[:, t, :], dt[t][:], ACT.Copy, scale=gb_signed[:, t : t + 1])
        z2_grouped = keep.tile([P, PACK * N], BF16, name="z2_grouped", align_bytes=64)
        nc.scalar.copy(
            z2_grouped[:].rearrange("p (c i t) -> p c t i", i=4, t=PACK),
            z2_planes[:].rearrange("p t (c i) -> p c t i", i=4),
        )

        first = keep.tile([P, PACK, N], F32, name="first")
        second = keep.tile([P, PACK, N], F32, name="second")
        for t in range(PACK):
            y1 = keep.tile([P, N], F32, name="y1_%d" % t, tag="y1_%d" % t, align_bytes=64)
            y2 = keep.tile([P, N], F32, name="y2_%d" % t)
            nc.vector.tensor_copy(y1[:], y[t][:].indirect(l1[:]))
            nc.vector.tensor_copy(y2[:], y[t][:].indirect(l2[:]))
            nc.vector.tensor_tensor(first[:, t, :], d[t][:].indirect(l3[:]), y1[:], ALU.add)
            nc.vector.tensor_tensor(second[:, t, :], d[t][:].indirect(l4[:]), y2[:], ALU.add)

        qz2 = quantise(z2_grouped, "moving", tag="y1_3")

        first_v = first[:].rearrange("p t (g u r) -> p u g t r", u=4, r=4)
        second_v = second[:].rearrange("p t (g u r) -> p u g t r", u=4, r=4)
        z_grouped = []

        def larger_sum(u):
            zg = keep.tile([P, N], BF16, name="z_grouped%d" % u, align_bytes=64)
            nc.vector.tensor_tensor(
                zg[:].rearrange("p (g r t) -> p g t r", r=4, t=PACK), first_v[:, u], second_v[:, u], ALU.max
            )
            z_grouped.append(zg)

        larger_sum(0)
        out_v = out.rearrange("(g u r) v -> u g r v", u=4, r=4)
        scores = []
        for u in range(4):
            if u + 1 < 4:
                larger_sum(u + 1)
            qz = quantise(z_grouped[u], "qz%d" % u)
            acc = product(qz, slice(0, P), qz2)
            s = keep.tile([P, WIDE], F32, name="s%d" % u)
            nc.scalar.mul(s[:, :N], acc[:], 0.0625)
            gate = keep.tile([P, N], F32, name="gate%d" % u)
            scores.append((s, gate))
            if u > 0:
                nc.scalar.activation(scores[u - 1][1][:], scores[u - 1][0][:].indirect(l7[:]), ACT.Sigmoid)
        nc.scalar.activation(scores[3][1][:], scores[3][0][:].indirect(l7[:]), ACT.Sigmoid)
        fetched, gated = [], []

        def fetch(u):
            tile = keep.tile([P, N], F32, name="fetched%d" % u)
            nc.vector.tensor_copy(tile[:], scores[u][0][:].indirect(l8[:]))
            fetched.append(tile)

        def gate_scores(u, parts):
            tile = keep.tile([P, N], F32, name="gated%d" % u)
            for c in range(0, N, N // parts):
                cols = slice(c, c + N // parts)
                nc.vector.tensor_tensor(tile[:, cols], scores[u][0][:, cols], scores[u][1][:, cols], ALU.mult)
            gated.append(tile)

        def finish(u, parts):
            res = keep.tile([P, N], F32, name="res%d" % u)
            for c in range(0, N, N // parts):
                cols = slice(c, c + N // parts)
                nc.vector.tensor_tensor(res[:, cols], gated[u][:, cols], fetched[u][:, cols], ALU.max)
                nc.sync.dma_start(out=out_v[u][:, :, cols], in_=res[:, cols])

        fetch(0)
        for u in range(3):
            gate_scores(u, 1)
            fetch(u + 1)
            finish(u, 1)
        gate_scores(3, 2)
        finish(3, 2)
